import numpy as np
import ml_dtypes


def mxq(x, axis, fmt="e4m3"):
    dtype, down = {"e4m3": (ml_dtypes.float8_e4m3fn, 7), "e5m2": (ml_dtypes.float8_e5m2, 14)}[fmt]
    v = np.moveaxis(np.asarray(x, np.float32).astype(ml_dtypes.bfloat16).astype(np.float64), axis, -1)
    blocks = v.reshape(v.shape[:-1] + (-1, 32))
    amax = np.abs(blocks).max(-1, keepdims=True)
    byte = np.maximum(np.where(amax > 0, np.frexp(amax)[1] - 1 + 127, 0) - down, 1)
    scale = np.exp2(byte - 127.0)
    codes = (blocks / scale).astype(np.float32).astype(dtype).astype(np.float64)
    return np.moveaxis((codes * scale).reshape(v.shape), -1, axis)


WIDE = False


def mx_kscale(k):
    if not WIDE:
        return np.ones(k)
    levels = np.array([10, -10, 5, -5, 0])
    if k % 512:
        return np.exp2(np.random.permutation(np.resize(levels, k // 32))).repeat(32)
    a = np.empty((k // 512, 16))
    for p in range(k // 512):
        a[p, :8] = np.random.permutation(np.resize(levels, 8))
        for g in range(8):
            far = levels[np.abs(levels - a[p, g]) >= 10]
            a[p, g + 8] = far[np.random.randint(len(far))]
    return np.exp2(a.ravel()).repeat(32)


def f64(x):
    return np.asarray(x).astype(np.float64)


def striped(idx):
    return np.tile(np.asarray(idx).reshape(-1, 16).T, (8, 1)).astype(np.uint16)


def unstriped(offs):
    return offs[:16].T.reshape(-1).astype(np.int64)


E2M1 = np.array([0.0, 0.5, 1.0, 1.5, 2.0, 3.0, 4.0, 6.0, -0.0, -0.5, -1.0, -1.5, -2.0, -3.0, -4.0, -6.0])


def pack_weight(w, fmt):
    k, n = w.shape
    w = f64(np.asarray(w, np.float32).astype(ml_dtypes.bfloat16)).reshape(k // 32, 32, n)
    amax = np.abs(w).max(1)
    if fmt == "e4m3":
        byte = np.frexp(amax)[1] - 1 + 127 - 7
    else:
        mant, ex = np.frexp(amax / 6.0)
        byte = np.where(mant > 0.5, ex, ex - 1) + 127
    byte = np.clip(np.where(amax > 0, byte, 1), 1, 254)
    scaled = (w * np.exp2(127.0 - byte)[:, None, :]).reshape(k, n).astype(np.float32)
    by_word = np.ascontiguousarray(scaled.reshape(k // 512, 128, 4, n).transpose(0, 1, 3, 2))
    if fmt == "e4m3":
        words = by_word.astype(ml_dtypes.float8_e4m3fn).view(np.uint8)
    else:
        c = by_word.astype(ml_dtypes.float4_e2m1fn).view(np.uint8) & 0xF
        words = (c[..., 0::2] | (c[..., 1::2] << 4)).reshape(k // 512, 128, 2 * n)
    return np.ascontiguousarray(words), np.ascontiguousarray(byte.astype(np.uint8).reshape(k // 512, 16, n))


def unpack_weight(words, scales, fmt):
    g, _, n = scales.shape
    words = np.ascontiguousarray(words).reshape(g, 128, n, -1)
    if fmt == "e4m3":
        vals = words.view(ml_dtypes.float8_e4m3fn).astype(np.float64)
    else:
        nib = np.empty((g, 128, n, 4), np.uint8)
        nib[..., 0::2] = words & 0xF
        nib[..., 1::2] = words >> 4
        vals = E2M1[nib]
    vals = vals * np.repeat(np.exp2(scales.astype(np.float64) - 127.0), 8, axis=1)[..., None]
    return vals.transpose(0, 1, 3, 2).reshape(g * 512, n)


D, T, I, Q, E, Z, M, C = 512, 2048, 512, 256, 512, 1024, 1024, 512


def setup_inputs():
    n = np.random.standard_normal
    idx = np.random.permutation(T)[:I]
    idx2 = np.random.permutation(Z)[:I]
    idx3 = np.random.permutation(M)[:Q]
    fd = mx_kscale(D)
    fi = mx_kscale(I)
    fc = mx_kscale(C)
    ti = np.ones(T)
    ti[idx] = fi
    keysp = pack_weight(n((D, T)) / fd[:, None], "e4m3")
    return {
        "query": (n((D, Q)) * 1.0 / np.sqrt(D) * fd[:, None]).astype(np.float32),
        "query2": (n((D, Q)) * 1.0 / np.sqrt(D) * fd[:, None]).astype(np.float32),
        "keys_words": keysp[0],
        "keys_scales": keysp[1],
        "pages": (n((D, Z)) / fd[:, None]).astype(np.float32),
        "os": (np.random.uniform(0.02, 0.08, (1, I)) * fi).astype(np.float32),
        "vals": (n((E, T)) / ti).astype(np.float32),
        "wm": (n((C, E)) * 1.0 / np.sqrt(C) * fc[:, None]).astype(np.float32),
        "mstore": (n((C, M)) / fc[:, None]).astype(np.float32),
        "offs": striped(idx),
        "offs2": striped(idx2),
        "offs3": striped(idx3),
    }


def reference(query, query2, keys_words, keys_scales, pages, os, vals, wm, mstore, offs, offs2, offs3):
    idx = unstriped(offs)
    idx2 = unstriped(offs2)
    idx3 = unstriped(offs3)
    keysu = unpack_weight(keys_words, keys_scales, "e4m3")
    queryq = mxq(f64(query), 0, "e4m3")
    keysidxg = keysu[:, idx]
    a = queryq.T @ keysidxg
    query2q = mxq(f64(query2), 0, "e4m3")
    pagesq = mxq(f64(pages), 0, "e4m3")
    h0 = query2q.T @ pagesq
    s = np.maximum(a, h0[:, idx2])
    w = np.maximum(s, 0.0)
    wo1 = w * f64(os)
    wt1 = wo1.T
    vt1 = f64(vals)[:, idx].T
    vt1q = mxq(vt1, 0, "e4m3")
    wt1q = mxq(wt1, 0, "e4m3")
    wmq = mxq(f64(wm), 0, "e4m3")
    mstoreidx3q = mxq(f64(mstore)[:, idx3], 0, "e4m3")
    o = vt1q.T @ wt1q + wmq.T @ mstoreidx3q
    return o

@@ -1,0 +1,169 @@
+from contextlib import ExitStack
+
+import concourse.mybir as mybir
+from concourse.masks import make_identity
+
+D, T, I, Q, E, Z, M, C = 512, 2048, 512, 256, 512, 1024, 1024, 512
+FLOPS = 2 * (D * Q * I + D * Q * Z + I * E * Q + C * E * Q)
+
+F32 = mybir.dt.float32
+BF16 = mybir.dt.bfloat16
+I32 = mybir.dt.int32
+U32 = mybir.dt.uint32
+U16 = mybir.dt.uint16
+U8 = mybir.dt.uint8
+FP8X4 = mybir.dt.float8_e4m3fn_x4
+COPY = mybir.ActivationFunctionType.Copy
+MAX = mybir.AluOpType.max
+MULT = mybir.AluOpType.mult
+
+P = 128
+PACK = 4
+BANK = 512
+WM_EARLY = 384
+
+
+def tile_attend_widelarger_addedmemory_lean_kernel(
+    tc, query, query2, keys_words, keys_scales, pages, slot_factor, vals, wm, mstore, offs, offs2, offs3, out
+):
+    nc = tc.nc
+    q_tiles = Q // P
+    e_tiles = E // P
+
+    with ExitStack() as ctx:
+        sb = ctx.enter_context(tc.tile_pool(name="sb", bufs=1))
+        ps_wide = ctx.enter_context(tc.psum_pool(name="ps_wide", bufs=4))
+        ps_turn = ctx.enter_context(tc.psum_pool(name="ps_turn", bufs=2))
+        ps_out = ctx.enter_context(tc.psum_pool(name="ps_out", bufs=2))
+
+        def rows_by_four(src):
+            return src.rearrange("(p t) w -> p t w", t=PACK)
+
+        def load(name, shape, dtype, src):
+            tile = sb.tile(shape, dtype, name=name, tag=name, align_bytes=64)
+            nc.sync.dma_start(tile[:], src)
+            return tile
+
+        def interleave(name, planes, tag="staged"):
+            width = planes.shape[2]
+            grouped = sb.tile([P, width, PACK], BF16, name=name, tag=tag, align_bytes=64)
+            nc.vector.tensor_copy(out=grouped[:], in_=planes.rearrange("p t w -> p w t"))
+            return grouped
+
+        def quantize(name, grouped):
+            width = grouped.shape[1]
+            codes = sb.tile([P, width], U32, name=name + "_codes", tag=name + "_codes", align_bytes=64)
+            scales = sb.tile([P, width], U8, name=name + "_scales", align_bytes=64)
+            nc.vector.quantize_mx(
+                out=codes[:].bitcast(FP8X4), scales=scales[:], in_=grouped[:].rearrange("p w t -> p (w t)")
+            )
+            return codes, scales
+
+        def product(acc, stationary, s_cols, moving, start, stop):
+            nc.tensor.matmul_mx(
+                out=acc,
+                lhsT=stationary[0][:, s_cols].bitcast(FP8X4),
+                lhsT_scale=stationary[1][:, s_cols],
+                rhs=moving[0][:].bitcast(FP8X4),
+                rhs_scale=moving[1][:],
+                start=start,
+                stop=stop,
+            )
+
+        key_bytes = sb.tile([P, T], U8, name="key_bytes", align_bytes=64)
+        nc.gpsimd.memset(key_bytes[:].bitcast(U32), 0)
+        ident = sb.tile([P, P], F32, name="ident")
+        make_identity(nc, ident[:])
+
+        def pages_half(h):
+            return load("pages_raw%d" % h, [P, PACK, BANK], F32, rows_by_four(pages)[:, :, h * BANK : (h + 1) * BANK])
+
+        query2_raw = load("query2_raw", [P, PACK, Q], F32, rows_by_four(query2))
+        list1 = load("list1", [P, I // 16], U16, offs)
+        for quad in range(4):
+            nc.sync.dma_start(
+                key_bytes[32 * quad : 32 * quad + 4, :].bitcast(I32),
+                keys_scales[0, 4 * quad : 4 * quad + 4, :].bitcast(I32),
+            )
+        pages_raw = [pages_half(h) for h in range(Z // BANK)]
+        list2 = load("list2", [P, I // 16], U16, offs2)
+        query_raw = load("query_raw", [P, PACK, Q], F32, rows_by_four(query))
+        key_words = sb.tile([P, T], U32, name="key_words", align_bytes=64)
+        nc.sync.dma_start(key_words[:].bitcast(I32), keys_words[0].rearrange("p n t -> p (n t)").bitcast(I32))
+        list3 = load("list3", [P, Q // 16], U16, offs3)
+        os_cols = load("os_cols", [P, PACK], F32, slot_factor.rearrange("o (p t) -> (o p) t", t=PACK))
+        store_raw = [load("store_raw%d" % t, [P, M], F32, rows_by_four(mstore)[:, t, :]) for t in range(PACK)]
+        wm_early = load("wm_early", [P, PACK, WM_EARLY], F32, rows_by_four(wm)[:, :, :WM_EARLY])
+        vals_raw = [load("vals_raw%d" % j, [P, T], F32, vals[j * P : (j + 1) * P, :]) for j in range(e_tiles)]
+        wm_late = load("wm_late", [P, PACK, E - WM_EARLY], F32, rows_by_four(wm)[:, :, WM_EARLY:])
+
+        query2_g = interleave("query2_g", query2_raw[:])
+        query2_q = quantize("query2", query2_g)
+        listed_words = sb.tile([P, I], U32, name="listed_words", align_bytes=64)
+        listed_bytes = sb.tile([P, I], U8, name="listed_bytes", align_bytes=64)
+        nc.vector.tensor_copy(listed_bytes[:], key_bytes[:].indirect(list1[:]))
+        h0 = [sb.tile([P, Z], F32, name="h0_%d" % a, tag="h0_%d" % a, align_bytes=64) for a in range(q_tiles)]
+        for h in range(Z // BANK):
+            pages_q = quantize("pages%d" % h, interleave("pages_g%d" % h, pages_raw[h][:]))
+            for a in range(q_tiles):
+                acc = ps_wide.tile([P, BANK], F32, name="wide")
+                product(acc[:], query2_q, slice(a * P, (a + 1) * P), pages_q, True, True)
+                nc.scalar.copy(out=h0[a][:, h * BANK : (h + 1) * BANK], in_=acc[:])
+        query_g = sb.tile([P, Q, PACK], BF16, name="query_g", align_bytes=64)
+        nc.scalar.copy(out=query_g[:], in_=query_raw[:].rearrange("p t w -> p w t"))
+        query_q = quantize("query", query_g)
+        h0_listed = [sb.tile([P, I], F32, name="h0_listed%d" % a, align_bytes=64) for a in range(q_tiles)]
+        for a in range(q_tiles):
+            nc.scalar.activation(h0_listed[a][:], h0[a][:].indirect(list2[:]), COPY)
+
+        nc.vector.tensor_copy(listed_words[:], key_words[:].indirect(list1[:]))
+        weights_g = sb.tile([P, Q, PACK], BF16, name="weights_g", tag="staged", align_bytes=64)
+        weights = [sb.tile([P, I], F32, name="weights%d" % a, align_bytes=64) for a in range(q_tiles)]
+        for a in range(q_tiles):
+            acc = ps_wide.tile([P, BANK], F32, name="wide")
+            product(acc[:], query_q, slice(a * P, (a + 1) * P), (listed_words, listed_bytes), True, True)
+            nc.vector.scalar_tensor_tensor(weights[a][:], acc[:], 0.0, h0_listed[a][:], MAX, MAX)
+        for a in range(q_tiles):
+            turned = ps_wide.tile([P, BANK], F32, name="wide")
+            for t in range(PACK):
+                nc.tensor.transpose(turned[:, t * P : (t + 1) * P], weights[a][:, t:I:PACK], ident[:])
+            nc.vector.tensor_tensor(
+                weights_g[:, a * P : (a + 1) * P, :],
+                turned[:].rearrange("p (t q) -> p q t", t=PACK),
+                os_cols[:].unsqueeze(1).to_broadcast([P, P, PACK]),
+                MULT,
+            )
+        weights_q = quantize("weights", weights_g)
+
+        store_listed = sb.tile([P, PACK, Q], BF16, name="store_listed", tag="h0_1", align_bytes=64)
+        for t in range(PACK):
+            nc.scalar.activation(store_listed[:, t, :], store_raw[t][:].indirect(list3[:]), COPY)
+        store_q = quantize("store", interleave("store_g", store_listed[:]))
+
+
+        sums = []
+
+        def hand_out(j, tag):
+            result = sb.tile([P, Q], F32, name="result%d" % j, tag=tag, align_bytes=64)
+            nc.scalar.copy(out=result[:], in_=sums[j][:])
+            nc.sync.dma_start(out[j * P : (j + 1) * P, :], result[:])
+
+        for j in range(e_tiles):
+            listed = sb.tile([P, I], BF16, name="vals_listed%d" % j, tag="store_raw%d" % (PACK - 1 - j), align_bytes=64)
+            nc.scalar.activation(listed[:], vals_raw[j][:].indirect(list1[:]), COPY)
+            if j > 0:
+                hand_out(j - 1, "vals_raw%d" % j)
+            planes = wm_late[:] if j == e_tiles - 1 else wm_early[:, :, j * P : (j + 1) * P]
+            wm_q = quantize("wm%d" % j, interleave("wm_g%d" % j, planes))
+            pairs = listed[:].bitcast(F32)
+            turned = ps_turn.tile([P, 2, P], F32, name="turned_pairs")
+            for u in range(2):
+                nc.tensor.transpose(turned[:, u, :], pairs[:, u : I // 2 : 2], ident[:])
+            vals_g = sb.tile([P, P, PACK], BF16, name="vals_g%d" % j, tag="staged", align_bytes=64)
+            nc.vector.tensor_copy(out=vals_g[:].bitcast(F32), in_=turned[:].rearrange("p u e -> p e u"))
+            vals_q = quantize("vals%d" % j, vals_g)
+            acc = ps_out.tile([P, Q], F32, name="acc_out")
+            product(acc[:], wm_q, slice(0, P), store_q, True, False)
+            product(acc[:], vals_q, slice(0, P), weights_q, False, True)
+            sums.append(acc)
+        hand_out(e_tiles - 1, "result_last")

@@ -20,7 +20,8 @@ MULT = mybir.AluOpType.mult
 P = 128
 PACK = 4
 BANK = 512
-WM_EARLY = 384
+PAIR_BANKS = (4, 5, 0, 1)
+SUM_BANKS = (5, 0, 1, 2)
 
 
 def tile_attend_widelarger_addedmemory_lean_kernel(
@@ -32,9 +33,10 @@ def tile_attend_widelarger_addedmemory_lean_kernel(
 
     with ExitStack() as ctx:
         sb = ctx.enter_context(tc.tile_pool(name="sb", bufs=1))
-        ps_wide = ctx.enter_context(tc.psum_pool(name="ps_wide", bufs=4))
-        ps_turn = ctx.enter_context(tc.psum_pool(name="ps_turn", bufs=2))
-        ps_out = ctx.enter_context(tc.psum_pool(name="ps_out", bufs=2))
+        ps = ctx.enter_context(tc.psum_pool(name="ps", bufs=1))
+
+        def bank(number, name, shape):
+            return ps.tile(shape, F32, name=name, tag="bank%d" % number)
 
         def rows_by_four(src):
             return src.rearrange("(p t) w -> p t w", t=PACK)
@@ -44,18 +46,18 @@ def tile_attend_widelarger_addedmemory_lean_kernel(
             nc.sync.dma_start(tile[:], src)
             return tile
 
-        def interleave(name, planes, tag="staged"):
+        def interleave(name, planes, tag, copy):
             width = planes.shape[2]
             grouped = sb.tile([P, width, PACK], BF16, name=name, tag=tag, align_bytes=64)
-            nc.vector.tensor_copy(out=grouped[:], in_=planes.rearrange("p t w -> p w t"))
+            copy(out=grouped[:], in_=planes.rearrange("p t w -> p w t"))
             return grouped
 
-        def quantize(name, grouped):
+        def quantize(name, grouped, tag=None):
             width = grouped.shape[1]
-            codes = sb.tile([P, width], U32, name=name + "_codes", tag=name + "_codes", align_bytes=64)
+            codes = sb.tile([P, width], U32, name=name + "_codes", tag=tag or name + "_codes", align_bytes=64)
             scales = sb.tile([P, width], U8, name=name + "_scales", align_bytes=64)
             nc.vector.quantize_mx(
-                out=codes[:].bitcast(FP8X4), scales=scales[:], in_=grouped[:].rearrange("p w t -> p (w t)")
+                out=codes[:].bitcast(FP8X4), scales=scales[:], in_=grouped.rearrange("p w t -> p (w t)")
             )
             return codes, scales
 
@@ -71,60 +73,67 @@ def tile_attend_widelarger_addedmemory_lean_kernel(
             )
 
         key_bytes = sb.tile([P, T], U8, name="key_bytes", align_bytes=64)
-        nc.gpsimd.memset(key_bytes[:].bitcast(U32), 0)
+        nc.vector.memset(key_bytes[:].bitcast(I32), 0)
         ident = sb.tile([P, P], F32, name="ident")
         make_identity(nc, ident[:])
 
-        def pages_half(h):
-            return load("pages_raw%d" % h, [P, PACK, BANK], F32, rows_by_four(pages)[:, :, h * BANK : (h + 1) * BANK])
-
         query2_raw = load("query2_raw", [P, PACK, Q], F32, rows_by_four(query2))
         list1 = load("list1", [P, I // 16], U16, offs)
-        for quad in range(4):
-            nc.sync.dma_start(
-                key_bytes[32 * quad : 32 * quad + 4, :].bitcast(I32),
-                keys_scales[0, 4 * quad : 4 * quad + 4, :].bitcast(I32),
-            )
-        pages_raw = [pages_half(h) for h in range(Z // BANK)]
+        for r in range(4):
+            nc.sync.dma_start(key_bytes[r:P:32, :].bitcast(I32), keys_scales[0, r:16:4, :].bitcast(I32))
+        pages_raw = [
+            load("pages_raw%d" % h, [P, PACK, BANK], F32, rows_by_four(pages)[:, :, h * BANK : (h + 1) * BANK])
+            for h in range(Z // BANK)
+        ]
         list2 = load("list2", [P, I // 16], U16, offs2)
         query_raw = load("query_raw", [P, PACK, Q], F32, rows_by_four(query))
         key_words = sb.tile([P, T], U32, name="key_words", align_bytes=64)
         nc.sync.dma_start(key_words[:].bitcast(I32), keys_words[0].rearrange("p n t -> p (n t)").bitcast(I32))
-        list3 = load("list3", [P, Q // 16], U16, offs3)
         os_cols = load("os_cols", [P, PACK], F32, slot_factor.rearrange("o (p t) -> (o p) t", t=PACK))
-        store_raw = [load("store_raw%d" % t, [P, M], F32, rows_by_four(mstore)[:, t, :]) for t in range(PACK)]
-        wm_early = load("wm_early", [P, PACK, WM_EARLY], F32, rows_by_four(wm)[:, :, :WM_EARLY])
         vals_raw = [load("vals_raw%d" % j, [P, T], F32, vals[j * P : (j + 1) * P, :]) for j in range(e_tiles)]
-        wm_late = load("wm_late", [P, PACK, E - WM_EARLY], F32, rows_by_four(wm)[:, :, WM_EARLY:])
+        list3 = load("list3", [P, Q // 16], U16, offs3)
+        store_raw = [load("store_raw%d" % t, [P, M], F32, rows_by_four(mstore)[:, t, :]) for t in range(PACK)]
+        wm_raw = load("wm_raw", [P, PACK, E], F32, rows_by_four(wm))
 
-        query2_g = interleave("query2_g", query2_raw[:])
-        query2_q = quantize("query2", query2_g)
-        listed_words = sb.tile([P, I], U32, name="listed_words", align_bytes=64)
+        query2_q = quantize("query2", interleave("query2_g", query2_raw[:], "first", nc.vector.tensor_copy)[:])
         listed_bytes = sb.tile([P, I], U8, name="listed_bytes", align_bytes=64)
         nc.vector.tensor_copy(listed_bytes[:], key_bytes[:].indirect(list1[:]))
         h0 = [sb.tile([P, Z], F32, name="h0_%d" % a, tag="h0_%d" % a, align_bytes=64) for a in range(q_tiles)]
         for h in range(Z // BANK):
-            pages_q = quantize("pages%d" % h, interleave("pages_g%d" % h, pages_raw[h][:]))
+            pages_g = interleave("pages_g%d" % h, pages_raw[h][:], "first", nc.vector.tensor_copy)
+            pages_q = quantize("pages%d" % h, pages_g[:])
             for a in range(q_tiles):
-                acc = ps_wide.tile([P, BANK], F32, name="wide")
+                acc = bank(2 * h + a, "h0_sum%d_%d" % (h, a), [P, BANK])
                 product(acc[:], query2_q, slice(a * P, (a + 1) * P), pages_q, True, True)
                 nc.scalar.copy(out=h0[a][:, h * BANK : (h + 1) * BANK], in_=acc[:])
-        query_g = sb.tile([P, Q, PACK], BF16, name="query_g", align_bytes=64)
-        nc.scalar.copy(out=query_g[:], in_=query_raw[:].rearrange("p t w -> p w t"))
-        query_q = quantize("query", query_g)
+        query_q = quantize("query", interleave("query_g", query_raw[:], "first", nc.vector.tensor_copy)[:])
         h0_listed = [sb.tile([P, I], F32, name="h0_listed%d" % a, align_bytes=64) for a in range(q_tiles)]
-        for a in range(q_tiles):
-            nc.scalar.activation(h0_listed[a][:], h0[a][:].indirect(list2[:]), COPY)
+        nc.scalar.activation(h0_listed[0][:], h0[0][:].indirect(list2[:]), COPY)
 
+        listed_words = sb.tile([P, I], U32, name="listed_words", tag="first", align_bytes=64)
         nc.vector.tensor_copy(listed_words[:], key_words[:].indirect(list1[:]))
-        weights_g = sb.tile([P, Q, PACK], BF16, name="weights_g", tag="staged", align_bytes=64)
+        nc.vector.tensor_copy(h0_listed[1][:], h0[1][:].indirect(list2[:]))
         weights = [sb.tile([P, I], F32, name="weights%d" % a, align_bytes=64) for a in range(q_tiles)]
         for a in range(q_tiles):
-            acc = ps_wide.tile([P, BANK], F32, name="wide")
+            acc = bank(4 + a, "scores%d" % a, [P, BANK])
             product(acc[:], query_q, slice(a * P, (a + 1) * P), (listed_words, listed_bytes), True, True)
             nc.vector.scalar_tensor_tensor(weights[a][:], acc[:], 0.0, h0_listed[a][:], MAX, MAX)
+
+        def values_block(j):
+            tag = "vals_raw%d" % (j - 1) if j > 0 else "h0_0"
+            listed = sb.tile([P, I], BF16, name="vals_listed%d" % j, tag=tag, align_bytes=64)
+            nc.scalar.activation(listed[:], vals_raw[j][:].indirect(list1[:]), COPY)
+            pairs = listed[:].bitcast(F32)
+            turned = bank(PAIR_BANKS[j], "turned_pairs%d" % j, [P, 2, P])
+            for u in range(2):
+                nc.tensor.transpose(turned[:, u, :], pairs[:, u : I // 2 : 2], ident[:])
+            vals_g = sb.tile([P, P, PACK], BF16, name="vals_g%d" % j, tag="vals_g%d" % j, align_bytes=64)
+            nc.vector.tensor_copy(out=vals_g[:].bitcast(F32), in_=turned[:].rearrange("p u e -> p e u"))
+            return quantize("vals%d" % j, vals_g[:])
+
+        weights_g = sb.tile([P, Q, PACK], BF16, name="weights_g", tag="first", align_bytes=64)
         for a in range(q_tiles):
-            turned = ps_wide.tile([P, BANK], F32, name="wide")
+            turned = bank(6 + a, "weights_turned%d" % a, [P, BANK])
             for t in range(PACK):
                 nc.tensor.transpose(turned[:, t * P : (t + 1) * P], weights[a][:, t:I:PACK], ident[:])
             nc.vector.tensor_tensor(
@@ -133,37 +142,33 @@ def tile_attend_widelarger_addedmemory_lean_kernel(
                 os_cols[:].unsqueeze(1).to_broadcast([P, P, PACK]),
                 MULT,
             )
-        weights_q = quantize("weights", weights_g)
+        weights_q = quantize("weights", weights_g[:])
+        vals_qs = [values_block(j) for j in range(e_tiles)]
+        sums = []
+        for j in range(e_tiles):
+            acc = bank(SUM_BANKS[j], "sum%d" % j, [P, Q])
+            product(acc[:], vals_qs[j], slice(0, P), weights_q, True, False)
+            sums.append(acc)
 
-        store_listed = sb.tile([P, PACK, Q], BF16, name="store_listed", tag="h0_1", align_bytes=64)
+        store_listed = sb.tile([P, PACK, Q], BF16, name="store_listed", tag="vals_raw3", align_bytes=64)
         for t in range(PACK):
             nc.scalar.activation(store_listed[:, t, :], store_raw[t][:].indirect(list3[:]), COPY)
-        store_q = quantize("store", interleave("store_g", store_listed[:]))
+        store_q = quantize("store", interleave("store_g", store_listed[:], "vals_g3", nc.vector.tensor_copy)[:])
 
-
-        sums = []
-
-        def hand_out(j, tag):
-            result = sb.tile([P, Q], F32, name="result%d" % j, tag=tag, align_bytes=64)
-            nc.scalar.copy(out=result[:], in_=sums[j][:])
-            nc.sync.dma_start(out[j * P : (j + 1) * P, :], result[:])
-
+        wm_tags = ["vals_g3", "store_raw3"]
+        wm_copy = [nc.vector.tensor_copy, nc.scalar.copy]
+        wm_g = [
+            sb.tile([P, E // 2, PACK], BF16, name="wm_g%d" % h, tag=wm_tags[h], align_bytes=64) for h in range(2)
+        ]
         for j in range(e_tiles):
-            listed = sb.tile([P, I], BF16, name="vals_listed%d" % j, tag="store_raw%d" % (PACK - 1 - j), align_bytes=64)
-            nc.scalar.activation(listed[:], vals_raw[j][:].indirect(list1[:]), COPY)
-            if j > 0:
-                hand_out(j - 1, "vals_raw%d" % j)
-            planes = wm_late[:] if j == e_tiles - 1 else wm_early[:, :, j * P : (j + 1) * P]
-            wm_q = quantize("wm%d" % j, interleave("wm_g%d" % j, planes))
-            pairs = listed[:].bitcast(F32)
-            turned = ps_turn.tile([P, 2, P], F32, name="turned_pairs")
-            for u in range(2):
-                nc.tensor.transpose(turned[:, u, :], pairs[:, u : I // 2 : 2], ident[:])
-            vals_g = sb.tile([P, P, PACK], BF16, name="vals_g%d" % j, tag="staged", align_bytes=64)
-            nc.vector.tensor_copy(out=vals_g[:].bitcast(F32), in_=turned[:].rearrange("p u e -> p e u"))
-            vals_q = quantize("vals%d" % j, vals_g)
-            acc = ps_out.tile([P, Q], F32, name="acc_out")
-            product(acc[:], wm_q, slice(0, P), store_q, True, False)
-            product(acc[:], vals_q, slice(0, P), weights_q, False, True)
-            sums.append(acc)
-        hand_out(e_tiles - 1, "result_last")
+            wm_copy[j // 2](
+                out=wm_g[j // 2][:, j % 2 * P : (j % 2 + 1) * P, :],
+                in_=wm_raw[:, :, j * P : (j + 1) * P].rearrange("p t w -> p w t"),
+            )
+        for j in range(e_tiles):
+            wm_q = quantize("wm%d" % j, wm_g[j // 2][:, j % 2 * P : (j % 2 + 1) * P, :])
+            product(sums[j][:], wm_q, slice(0, P), store_q, False, True)
+        for j in range(e_tiles):
+            result = sb.tile([P, Q], F32, name="result%d" % j)
+            wm_copy[(j + 1) % 2](out=result[:], in_=sums[j][:])
+            nc.sync.dma_start(out[j * P : (j + 1) * P, :], result[:])

@@ -20,6 +20,7 @@ MULT = mybir.AluOpType.mult
 P = 128
 PACK = 4
 BANK = 512
+RUN = 4
 PAIR_BANKS = (4, 5, 0, 1)
 SUM_BANKS = (5, 0, 1, 2)
 
@@ -46,10 +47,16 @@ def tile_attend_widelarger_addedmemory_lean_kernel(
             nc.sync.dma_start(tile[:], src)
             return tile
 
+        def weave(copy, grouped, planes):
+            copy(
+                out=grouped.rearrange("p (c i) t -> p c t i", i=RUN),
+                in_=planes.rearrange("p t (c i) -> p c t i", i=RUN),
+            )
+
         def interleave(name, planes, tag, copy):
             width = planes.shape[2]
             grouped = sb.tile([P, width, PACK], BF16, name=name, tag=tag, align_bytes=64)
-            copy(out=grouped[:], in_=planes.rearrange("p t w -> p w t"))
+            weave(copy, grouped[:], planes)
             return grouped
 
         def quantize(name, grouped, tag=None):
@@ -81,10 +88,7 @@ def tile_attend_widelarger_addedmemory_lean_kernel(
         list1 = load("list1", [P, I // 16], U16, offs)
         for r in range(4):
             nc.sync.dma_start(key_bytes[r:P:32, :].bitcast(I32), keys_scales[0, r:16:4, :].bitcast(I32))
-        pages_raw = [
-            load("pages_raw%d" % h, [P, PACK, BANK], F32, rows_by_four(pages)[:, :, h * BANK : (h + 1) * BANK])
-            for h in range(Z // BANK)
-        ]
+        pages_raw = load("pages_raw", [P, PACK, Z], F32, rows_by_four(pages))
         list2 = load("list2", [P, I // 16], U16, offs2)
         query_raw = load("query_raw", [P, PACK, Q], F32, rows_by_four(query))
         key_words = sb.tile([P, T], U32, name="key_words", align_bytes=64)
@@ -99,9 +103,12 @@ def tile_attend_widelarger_addedmemory_lean_kernel(
         listed_bytes = sb.tile([P, I], U8, name="listed_bytes", align_bytes=64)
         nc.vector.tensor_copy(listed_bytes[:], key_bytes[:].indirect(list1[:]))
         h0 = [sb.tile([P, Z], F32, name="h0_%d" % a, tag="h0_%d" % a, align_bytes=64) for a in range(q_tiles)]
+        pages_g = [
+            interleave("pages_g0", pages_raw[:, :, :BANK], "first", nc.vector.tensor_copy),
+            interleave("pages_g1", pages_raw[:, :, BANK:], "second", nc.scalar.copy),
+        ]
         for h in range(Z // BANK):
-            pages_g = interleave("pages_g%d" % h, pages_raw[h][:], "first", nc.vector.tensor_copy)
-            pages_q = quantize("pages%d" % h, pages_g[:])
+            pages_q = quantize("pages%d" % h, pages_g[h][:])
             for a in range(q_tiles):
                 acc = bank(2 * h + a, "h0_sum%d_%d" % (h, a), [P, BANK])
                 product(acc[:], query2_q, slice(a * P, (a + 1) * P), pages_q, True, True)
@@ -110,7 +117,7 @@ def tile_attend_widelarger_addedmemory_lean_kernel(
         h0_listed = [sb.tile([P, I], F32, name="h0_listed%d" % a, align_bytes=64) for a in range(q_tiles)]
         nc.scalar.activation(h0_listed[0][:], h0[0][:].indirect(list2[:]), COPY)
 
-        listed_words = sb.tile([P, I], U32, name="listed_words", tag="first", align_bytes=64)
+        listed_words = sb.tile([P, I], U32, name="listed_words", tag="second", align_bytes=64)
         nc.vector.tensor_copy(listed_words[:], key_words[:].indirect(list1[:]))
         nc.vector.tensor_copy(h0_listed[1][:], h0[1][:].indirect(list2[:]))
         weights = [sb.tile([P, I], F32, name="weights%d" % a, align_bytes=64) for a in range(q_tiles)]
@@ -153,7 +160,10 @@ def tile_attend_widelarger_addedmemory_lean_kernel(
         store_listed = sb.tile([P, PACK, Q], BF16, name="store_listed", tag="vals_raw3", align_bytes=64)
         for t in range(PACK):
             nc.scalar.activation(store_listed[:, t, :], store_raw[t][:].indirect(list3[:]), COPY)
-        store_q = quantize("store", interleave("store_g", store_listed[:], "vals_g3", nc.vector.tensor_copy)[:])
+        store_g = sb.tile([P, Q, PACK], BF16, name="store_g", tag="vals_g3", align_bytes=64)
+        for t in range(0, PACK, 2):
+            weave(nc.vector.tensor_copy, store_g[:, :, t : t + 2], store_listed[:, t : t + 2, :])
+        store_q = quantize("store", store_g[:])
 
         wm_tags = ["vals_g3", "store_raw3"]
         wm_copy = [nc.vector.tensor_copy, nc.scalar.copy]
@@ -161,10 +171,7 @@ def tile_attend_widelarger_addedmemory_lean_kernel(
             sb.tile([P, E // 2, PACK], BF16, name="wm_g%d" % h, tag=wm_tags[h], align_bytes=64) for h in range(2)
         ]
         for j in range(e_tiles):
-            wm_copy[j // 2](
-                out=wm_g[j // 2][:, j % 2 * P : (j % 2 + 1) * P, :],
-                in_=wm_raw[:, :, j * P : (j + 1) * P].rearrange("p t w -> p w t"),
-            )
+            weave(wm_copy[j // 2], wm_g[j // 2][:, j % 2 * P : (j % 2 + 1) * P, :], wm_raw[:, :, j * P : (j + 1) * P])
         for j in range(e_tiles):
             wm_q = quantize("wm%d" % j, wm_g[j // 2][:, j % 2 * P : (j % 2 + 1) * P, :])
             product(sums[j][:], wm_q, slice(0, P), store_q, False, True)

from contextlib import ExitStack

import concourse.mybir as mybir
from concourse.masks import make_identity

D, T, I, Q, E, Z, M, C = 512, 2048, 512, 256, 512, 1024, 1024, 512
FLOPS = 2 * (D * Q * I + D * Q * Z + I * E * Q + C * E * Q)

F32 = mybir.dt.float32
BF16 = mybir.dt.bfloat16
I32 = mybir.dt.int32
U32 = mybir.dt.uint32
U16 = mybir.dt.uint16
U8 = mybir.dt.uint8
FP8X4 = mybir.dt.float8_e4m3fn_x4
COPY = mybir.ActivationFunctionType.Copy
MAX = mybir.AluOpType.max
MULT = mybir.AluOpType.mult

P = 128
PACK = 4
BANK = 512
RUN = 4
PAIR_BANKS = (4, 5, 0, 1)
SUM_BANKS = (5, 0, 1, 2)


def tile_attend_widelarger_addedmemory_lean_kernel(
    tc, query, query2, keys_words, keys_scales, pages, slot_factor, vals, wm, mstore, offs, offs2, offs3, out
):
    nc = tc.nc
    q_tiles = Q // P
    e_tiles = E // P

    with ExitStack() as ctx:
        sb = ctx.enter_context(tc.tile_pool(name="sb", bufs=1))
        ps = ctx.enter_context(tc.psum_pool(name="ps", bufs=1))

        def bank(number, name, shape):
            return ps.tile(shape, F32, name=name, tag="bank%d" % number)

        def rows_by_four(src):
            return src.rearrange("(p t) w -> p t w", t=PACK)

        def load(name, shape, dtype, src):
            tile = sb.tile(shape, dtype, name=name, tag=name, align_bytes=64)
            nc.sync.dma_start(tile[:], src)
            return tile

        def weave(copy, grouped, planes):
            copy(
                out=grouped.rearrange("p (c i) t -> p c t i", i=RUN),
                in_=planes.rearrange("p t (c i) -> p c t i", i=RUN),
            )

        def interleave(name, planes, tag, copy):
            width = planes.shape[2]
            grouped = sb.tile([P, width, PACK], BF16, name=name, tag=tag, align_bytes=64)
            weave(copy, grouped[:], planes)
            return grouped

        def quantize(name, grouped, tag=None):
            width = grouped.shape[1]
            codes = sb.tile([P, width], U32, name=name + "_codes", tag=tag or name + "_codes", align_bytes=64)
            scales = sb.tile([P, width], U8, name=name + "_scales", align_bytes=64)
            nc.vector.quantize_mx(
                out=codes[:].bitcast(FP8X4), scales=scales[:], in_=grouped.rearrange("p w t -> p (w t)")
            )
            return codes, scales

        def product(acc, stationary, s_cols, moving, start, stop):
            nc.tensor.matmul_mx(
                out=acc,
                lhsT=stationary[0][:, s_cols].bitcast(FP8X4),
                lhsT_scale=stationary[1][:, s_cols],
                rhs=moving[0][:].bitcast(FP8X4),
                rhs_scale=moving[1][:],
                start=start,
                stop=stop,
            )

        key_bytes = sb.tile([P, T], U8, name="key_bytes", align_bytes=64)
        nc.vector.memset(key_bytes[:].bitcast(I32), 0)
        ident = sb.tile([P, P], F32, name="ident")
        make_identity(nc, ident[:])

        query2_raw = load("query2_raw", [P, PACK, Q], F32, rows_by_four(query2))
        list1 = load("list1", [P, I // 16], U16, offs)
        for r in range(4):
            nc.sync.dma_start(key_bytes[r:P:32, :].bitcast(I32), keys_scales[0, r:16:4, :].bitcast(I32))
        pages_raw = load("pages_raw", [P, PACK, Z], F32, rows_by_four(pages))
        list2 = load("list2", [P, I // 16], U16, offs2)
        query_raw = load("query_raw", [P, PACK, Q], F32, rows_by_four(query))
        key_words = sb.tile([P, T], U32, name="key_words", align_bytes=64)
        nc.sync.dma_start(key_words[:].bitcast(I32), keys_words[0].rearrange("p n t -> p (n t)").bitcast(I32))
        os_cols = load("os_cols", [P, PACK], F32, slot_factor.rearrange("o (p t) -> (o p) t", t=PACK))
        vals_raw = [load("vals_raw%d" % j, [P, T], F32, vals[j * P : (j + 1) * P, :]) for j in range(e_tiles)]
        list3 = load("list3", [P, Q // 16], U16, offs3)
        store_raw = [load("store_raw%d" % t, [P, M], F32, rows_by_four(mstore)[:, t, :]) for t in range(PACK)]
        wm_raw = load("wm_raw", [P, PACK, E], F32, rows_by_four(wm))

        query2_q = quantize("query2", interleave("query2_g", query2_raw[:], "first", nc.vector.tensor_copy)[:])
        listed_bytes = sb.tile([P, I], U8, name="listed_bytes", align_bytes=64)
        nc.vector.tensor_copy(listed_bytes[:], key_bytes[:].indirect(list1[:]))
        h0 = [sb.tile([P, Z], F32, name="h0_%d" % a, tag="h0_%d" % a, align_bytes=64) for a in range(q_tiles)]
        pages_g = [
            interleave("pages_g0", pages_raw[:, :, :BANK], "first", nc.vector.tensor_copy),
            interleave("pages_g1", pages_raw[:, :, BANK:], "second", nc.scalar.copy),
        ]
        for h in range(Z // BANK):
            pages_q = quantize("pages%d" % h, pages_g[h][:])
            for a in range(q_tiles):
                acc = bank(2 * h + a, "h0_sum%d_%d" % (h, a), [P, BANK])
                product(acc[:], query2_q, slice(a * P, (a + 1) * P), pages_q, True, True)
                nc.scalar.copy(out=h0[a][:, h * BANK : (h + 1) * BANK], in_=acc[:])
        query_q = quantize("query", interleave("query_g", query_raw[:], "first", nc.vector.tensor_copy)[:])
        h0_listed = [sb.tile([P, I], F32, name="h0_listed%d" % a, align_bytes=64) for a in range(q_tiles)]
        nc.scalar.activation(h0_listed[0][:], h0[0][:].indirect(list2[:]), COPY)

        listed_words = sb.tile([P, I], U32, name="listed_words", tag="second", align_bytes=64)
        nc.vector.tensor_copy(listed_words[:], key_words[:].indirect(list1[:]))
        nc.vector.tensor_copy(h0_listed[1][:], h0[1][:].indirect(list2[:]))
        weights = [sb.tile([P, I], F32, name="weights%d" % a, align_bytes=64) for a in range(q_tiles)]
        for a in range(q_tiles):
            acc = bank(4 + a, "scores%d" % a, [P, BANK])
            product(acc[:], query_q, slice(a * P, (a + 1) * P), (listed_words, listed_bytes), True, True)
            nc.vector.scalar_tensor_tensor(weights[a][:], acc[:], 0.0, h0_listed[a][:], MAX, MAX)

        def values_block(j):
            tag = "vals_raw%d" % (j - 1) if j > 0 else "h0_0"
            listed = sb.tile([P, I], BF16, name="vals_listed%d" % j, tag=tag, align_bytes=64)
            nc.scalar.activation(listed[:], vals_raw[j][:].indirect(list1[:]), COPY)
            pairs = listed[:].bitcast(F32)
            turned = bank(PAIR_BANKS[j], "turned_pairs%d" % j, [P, 2, P])
            for u in range(2):
                nc.tensor.transpose(turned[:, u, :], pairs[:, u : I // 2 : 2], ident[:])
            vals_g = sb.tile([P, P, PACK], BF16, name="vals_g%d" % j, tag="vals_g%d" % j, align_bytes=64)
            nc.vector.tensor_copy(out=vals_g[:].bitcast(F32), in_=turned[:].rearrange("p u e -> p e u"))
            return quantize("vals%d" % j, vals_g[:])

        weights_g = sb.tile([P, Q, PACK], BF16, name="weights_g", tag="first", align_bytes=64)
        for a in range(q_tiles):
            turned = bank(6 + a, "weights_turned%d" % a, [P, BANK])
            for t in range(PACK):
                nc.tensor.transpose(turned[:, t * P : (t + 1) * P], weights[a][:, t:I:PACK], ident[:])
            nc.vector.tensor_tensor(
                weights_g[:, a * P : (a + 1) * P, :],
                turned[:].rearrange("p (t q) -> p q t", t=PACK),
                os_cols[:].unsqueeze(1).to_broadcast([P, P, PACK]),
                MULT,
            )
        weights_q = quantize("weights", weights_g[:])
        vals_qs = [values_block(j) for j in range(e_tiles)]
        sums = []
        for j in range(e_tiles):
            acc = bank(SUM_BANKS[j], "sum%d" % j, [P, Q])
            product(acc[:], vals_qs[j], slice(0, P), weights_q, True, False)
            sums.append(acc)

        store_listed = sb.tile([P, PACK, Q], BF16, name="store_listed", tag="vals_raw3", align_bytes=64)
        for t in range(PACK):
            nc.scalar.activation(store_listed[:, t, :], store_raw[t][:].indirect(list3[:]), COPY)
        store_g = sb.tile([P, Q, PACK], BF16, name="store_g", tag="vals_g3", align_bytes=64)
        for t in range(0, PACK, 2):
            weave(nc.vector.tensor_copy, store_g[:, :, t : t + 2], store_listed[:, t : t + 2, :])
        store_q = quantize("store", store_g[:])

        wm_tags = ["vals_g3", "store_raw3"]
        wm_copy = [nc.vector.tensor_copy, nc.scalar.copy]
        wm_g = [
            sb.tile([P, E // 2, PACK], BF16, name="wm_g%d" % h, tag=wm_tags[h], align_bytes=64) for h in range(2)
        ]
        for j in range(e_tiles):
            weave(wm_copy[j // 2], wm_g[j // 2][:, j % 2 * P : (j % 2 + 1) * P, :], wm_raw[:, :, j * P : (j + 1) * P])
        for j in range(e_tiles):
            wm_q = quantize("wm%d" % j, wm_g[j // 2][:, j % 2 * P : (j % 2 + 1) * P, :])
            product(sums[j][:], wm_q, slice(0, P), store_q, False, True)
        for j in range(e_tiles):
            result = sb.tile([P, Q], F32, name="result%d" % j)
            wm_copy[(j + 1) % 2](out=result[:], in_=sums[j][:])
            nc.sync.dma_start(out[j * P : (j + 1) * P, :], result[:])
